import numpy as np
import ml_dtypes


def mxq(x, axis, fmt="e4m3"):
    dtype, down = {"e4m3": (ml_dtypes.float8_e4m3fn, 7), "e5m2": (ml_dtypes.float8_e5m2, 14)}[fmt]
    v = np.moveaxis(np.asarray(x, np.float32).astype(ml_dtypes.bfloat16).astype(np.float64), axis, -1)
    blocks = v.reshape(v.shape[:-1] + (-1, 32))
    amax = np.abs(blocks).max(-1, keepdims=True)
    byte = np.maximum(np.where(amax > 0, np.frexp(amax)[1] - 1 + 127, 0) - down, 1)
    scale = np.exp2(byte - 127.0)
    codes = (blocks / scale).astype(np.float32).astype(dtype).astype(np.float64)
    return np.moveaxis((codes * scale).reshape(v.shape), -1, axis)


WIDE = False


def mx_kscale(k):
    if not WIDE:
        return np.ones(k)
    levels = np.array([10, -10, 5, -5, 0])
    if k % 512:
        return np.exp2(np.random.permutation(np.resize(levels, k // 32))).repeat(32)
    a = np.empty((k // 512, 16))
    for p in range(k // 512):
        a[p, :8] = np.random.permutation(np.resize(levels, 8))
        for g in range(8):
            far = levels[np.abs(levels - a[p, g]) >= 10]
            a[p, g + 8] = far[np.random.randint(len(far))]
    return np.exp2(a.ravel()).repeat(32)


def f64(x):
    return np.asarray(x).astype(np.float64)


def striped(idx):
    return np.tile(idx.reshape(-1, 16).T, (8, 1)).astype(np.uint16)


def unstriped(offs):
    return offs[:16].T.reshape(-1).astype(np.int64)


def striped8(idx):
    return np.concatenate([x.reshape(-1, 16).T for x in idx]).astype(np.uint16)


def runs(offs, k):
    lists = np.stack([offs[16 * r : 16 * r + 16].T.reshape(-1) for r in range(8)]).astype(np.int64)
    return lists[np.arange(k) % 512 // 64]


def pack_weight(w):
    k, n = w.shape
    w = f64(np.asarray(w, np.float32).astype(ml_dtypes.bfloat16)).reshape(k // 32, 32, n)
    amax = np.abs(w).max(1)
    byte = np.clip(np.where(amax > 0, np.frexp(amax)[1] - 1 + 127 - 7, 1), 1, 254)
    scaled = (w * np.exp2(127.0 - byte)[:, None, :]).reshape(k, n).astype(np.float32)
    words = np.ascontiguousarray(scaled.reshape(k // 512, 128, 4, n).transpose(0, 1, 3, 2)).astype(ml_dtypes.float8_e4m3fn).view(np.uint8)
    return words, np.ascontiguousarray(byte.astype(np.uint8).reshape(k // 512, 16, n))


def unpack_weight(words, scales):
    g, p, n, _ = words.shape
    vals = np.ascontiguousarray(words).view(ml_dtypes.float8_e4m3fn).astype(np.float64) * np.repeat(np.exp2(scales.astype(np.float64) - 127.0), 8, axis=1)[..., None]
    return vals.transpose(0, 1, 3, 2).reshape(g * 512, n)


def sigmoid(v):
    return 1.0 / (1.0 + np.exp(-np.maximum(v, -700.0)))


K, T, S, N, H = 512, 2048, 256, 512, 512


def setup_inputs():
    n = np.random.standard_normal
    s = mx_kscale(K)[:, None]
    u = mx_kscale(H)
    packed_xT = pack_weight(n((K, T)) * s)
    return {
        "x_words": packed_xT[0],
        "x_scales": packed_xT[1],
        "w1": (n((K, H)) / np.sqrt(K) / s).astype(np.float32),
        "gn": (np.random.uniform(0.5, 1.5, (H, 1)) * u[:, None]).astype(np.float32),
        "w2": (n((H, N)) / np.sqrt(H) / u[:, None]).astype(np.float32),
        "w3": (n((K, N)) / np.sqrt(K) / s).astype(np.float32),
        "offs": striped(np.random.permutation(T)[:S]),
        "n1": striped8(np.stack([np.random.permutation(S) for _ in range(8)])),
        "n2": striped8(np.stack([np.random.permutation(S) for _ in range(8)])),
        "two": striped(np.random.permutation(T)[:S]),
        "n3": striped8(np.stack([np.random.permutation(S) for _ in range(8)])),
        "n4": striped8(np.stack([np.random.permutation(S) for _ in range(8)])),
    }


def reference(x_words, x_scales, w1, gn, w2, w3, offs, n1, n2, two, n3, n4):
    xq = unpack_weight(x_words, x_scales)[:, unstriped(offs)]
    y = mxq(f64(w1), 0, "e4m3").T @ xq
    st = y - (y[np.arange(H)[:, None], runs(n1, H)])
    z = f64(gn) * (st / (np.abs(st[np.arange(H)[:, None], runs(n2, H)]) + 0.5))
    h = mxq(f64(w2), 0, "e4m3").T @ mxq(z, 0, "e4m3")
    x_two = unpack_weight(x_words, x_scales)[:, unstriped(two)]
    d = mxq(f64(w3), 0, "e4m3").T @ x_two
    return h + (sigmoid(d[np.arange(N)[:, None], runs(n4, N)] - d)) * (h[np.arange(N)[:, None], runs(n3, N)] - h)

@@ -1,0 +1,197 @@
+from contextlib import ExitStack
+
+import concourse.mybir as mybir
+
+K, T, S, N, H = 512, 2048, 256, 512, 512
+FLOPS = 3 * 2 * 512 * 512 * S
+
+F32 = mybir.dt.float32
+BF16 = mybir.dt.bfloat16
+I32 = mybir.dt.int32
+U32 = mybir.dt.uint32
+U16 = mybir.dt.uint16
+U8 = mybir.dt.uint8
+FP8X4 = mybir.dt.float8_e4m3fn_x4
+ALU = mybir.AluOpType
+ACT = mybir.ActivationFunctionType
+
+P = 128
+PACK = 4
+WINDOW = 2 * S
+LN_FLOOR = 2.0 ** -64
+
+
+def tile_picked_latepullbhopn_none_p_kernel(
+    tc, x_words, x_scales, w1, gn, w2, w3, offs, n1, n2, two, n3, n4, out
+):
+    nc = tc.nc
+    with ExitStack() as ctx:
+        keep = ctx.enter_context(tc.tile_pool(name="keep", bufs=1))
+        psum = ctx.enter_context(tc.psum_pool(name="psum", bufs=1))
+
+        def load_list(name, src):
+            tile = keep.tile([P, S // 16], U16, name=name)
+            nc.sync.dma_start(tile[:], src)
+            return tile
+
+        def load_weight(name, src):
+            raw = keep.tile([P, PACK, 512], F32, name=name)
+            nc.sync.dma_start(raw[:], src.rearrange("(p j) c -> p j c", j=PACK))
+            return raw
+
+        def windows(name):
+            return [keep.tile([P, WINDOW], F32, name="%s%d" % (name, t)) for t in range(PACK)]
+
+        def dealt_tile(name, tag):
+            return keep.tile([P, PACK, P, PACK], BF16, name=name, tag=tag, align_bytes=64)
+
+        def deal(dealt, raw, half, copy):
+            copy(
+                dealt.rearrange("p t m j -> p m j t"),
+                raw[:].rearrange("p j (m t) -> p m j t", t=PACK)[:, :, :, 2 * half : 2 * half + 2],
+            )
+            return dealt
+
+        def quantize(name, values, width):
+            codes = keep.tile([P, width], U32, name=name + "_codes", align_bytes=64)
+            scales = keep.tile([P, width], U8, name=name + "_scales", align_bytes=64)
+            nc.vector.quantize_mx(out=codes[:].bitcast(FP8X4), scales=scales[:], in_=values)
+            return codes, scales
+
+        def quantize_half(name, dealt, half):
+            return quantize("%s_%d" % (name, half), dealt.rearrange("p t m j -> p (t m j)"), 2 * P)
+
+        def product(acc, halves, t, moving):
+            codes, scales = halves[t // 2]
+            cols = slice(t % 2 * P, (t % 2 + 1) * P)
+            nc.tensor.matmul_mx(
+                out=acc,
+                lhsT=codes[:, cols].bitcast(FP8X4),
+                lhsT_scale=scales[:, cols],
+                rhs=moving[0][:].bitcast(FP8X4),
+                rhs_scale=moving[1][:],
+                start=True,
+                stop=True,
+            )
+
+        def fetch(dst, window, places, func, **kwargs):
+            nc.scalar.activation(dst, window[:].indirect(places[:]), func, **kwargs)
+
+        x_bytes = keep.tile([P, T], U8, name="x_bytes")
+        nc.vector.memset(x_bytes[:].bitcast(I32), 0)
+        gain = keep.tile([P, PACK], F32, name="gain")
+        nc.sync.dma_start(gain[:], gn.rearrange("(p t) o -> p (t o)", t=PACK))
+        w1_raw = load_weight("w1_raw", w1)
+        for q in range(4):
+            nc.sync.dma_start(
+                x_bytes[32 * q : 32 * q + 4, :].bitcast(I32), x_scales[0, 4 * q : 4 * q + 4, :].bitcast(I32)
+            )
+        offs_sb = load_list("offs_sb", offs)
+        x_packed = keep.tile([P, T], U32, name="x_packed")
+        nc.sync.dma_start(x_packed[:].bitcast(I32), x_words[0].rearrange("p n r -> p (n r)").bitcast(I32))
+        two_sb = load_list("two_sb", two)
+        n1_sb = load_list("n1_sb", n1)
+        w3_raw = load_weight("w3_raw", w3)
+        w2_raw = load_weight("w2_raw", w2)
+        n2_sb = load_list("n2_sb", n2)
+        n4_sb = load_list("n4_sb", n4)
+        n3_sb = load_list("n3_sb", n3)
+
+        y_win, ln_win, d_win, h_win = windows("y_win"), windows("ln_win"), windows("d_win"), windows("h_win")
+        for win in y_win + d_win + h_win:
+            nc.vector.memset(win[:, S:], 0.0)
+
+        gain_abs = keep.tile([P, PACK], F32, name="gain_abs")
+        gain_floor = keep.tile([P, PACK], F32, name="gain_floor")
+        gain_ln = keep.tile([P, PACK], F32, name="gain_ln")
+        gain_twice = keep.tile([P, PACK], F32, name="gain_twice")
+        gain_sign = keep.tile([P, PACK], F32, name="gain_sign")
+        nc.vector.scalar_tensor_tensor(gain_abs[:], gain[:], -1.0, gain[:], ALU.mult, ALU.max)
+        nc.vector.tensor_scalar(gain_floor[:], gain_abs[:], LN_FLOOR, None, ALU.max)
+        nc.scalar.activation(gain_ln[:], gain_floor[:], ACT.Ln)
+        nc.vector.tensor_scalar(gain_twice[:], gain[:], 0.0, 2.0, ALU.is_ge, ALU.mult)
+        nc.vector.tensor_scalar(gain_sign[:], gain_twice[:], -1.0, None, ALU.add)
+
+        def pick(name, dtype, table, places):
+            picked = keep.tile([P, S], dtype, name=name, align_bytes=64)
+            nc.vector.tensor_copy(picked[:], table[:].indirect(places[:]))
+            return picked
+
+        w1_dealt = []
+        for half, copy in enumerate((nc.vector.tensor_copy, nc.scalar.copy)):
+            dealt = keep.tile([P, 2, P, PACK], BF16, name="w1_dealt%d" % half, align_bytes=64)
+            w1_dealt.append(deal(dealt[:], w1_raw, half, copy))
+        offs_bytes = pick("offs_bytes", U8, x_bytes, offs_sb)
+        w1_q = [quantize_half("w1", w1_dealt[half], half) for half in range(2)]
+        two_bytes = pick("two_bytes", U8, x_bytes, two_sb)
+        offs_words = pick("offs_words", U32, x_packed, offs_sb)
+        y_acc = [psum.tile([P, S], F32, name="y_acc%d" % t) for t in range(PACK)]
+        y_far = keep.tile([P, PACK, S], F32, name="y_far", tag="y_far", align_bytes=64)
+        st = keep.tile([P, PACK, S], F32, name="st")
+        for t in range(PACK):
+            product(y_acc[t][:], w1_q, t, (offs_words, offs_bytes))
+        for t in range(PACK):
+            nc.vector.tensor_scalar(y_win[t][:, :S], y_acc[t][:], gain_sign[:, t : t + 1], None, ALU.mult)
+            fetch(y_far[:, t, :], y_win[t], n1_sb, ACT.Copy)
+        last = PACK - 1
+        for t in range(PACK):
+            nc.vector.tensor_tensor(st[:, t, :], y_win[t][:, :S], y_far[:, t, :], ALU.subtract)
+            if t < last:
+                nc.vector.scalar_tensor_tensor(ln_win[t][:, S:], st[:, t, :], -1.0, st[:, t, :], ALU.mult, ALU.max)
+            else:
+                nc.scalar.activation(ln_win[t][:, S:], st[:, t, :], ACT.Abs)
+            nc.scalar.activation(ln_win[t][:, :S], ln_win[t][:, S:], ACT.Ln, bias=0.5)
+        factor = keep.tile([P, PACK, S], F32, name="factor")
+        for t in range(PACK):
+            fetch(factor[:, t, :], ln_win[t], n2_sb, ACT.Exp, bias=gain_ln[:, t : t + 1], scale=-1.0)
+
+        two_words = pick("two_words", U32, x_packed, two_sb)
+        w3_tile = dealt_tile("w3_tile", "y_far")
+        w3_dealt = [deal(w3_tile[:, 2 * half : 2 * half + 2], w3_raw, half, nc.vector.tensor_copy) for half in range(2)]
+        w3_q = [quantize_half("w3", w3_dealt[half], half) for half in range(2)]
+        d_acc = [psum.tile([P, 2, S], F32, name="d_acc%d" % half) for half in range(2)]
+        for t in range(PACK):
+            product(d_acc[t // 2][:, t % 2, :], w3_q, t, (two_words, two_bytes))
+        d_far = keep.tile([P, PACK, S], F32, name="d_far")
+        for t in range(PACK):
+            nc.vector.tensor_copy(d_win[t][:, :S], d_acc[t // 2][:, t % 2, :])
+            fetch(d_far[:, t, :], d_win[t], n4_sb, ACT.Copy)
+
+        w2_tile = dealt_tile("w2_tile", "y_far")
+        w2_dealt = [deal(w2_tile[:, 2 * half : 2 * half + 2], w2_raw, half, nc.vector.tensor_copy) for half in range(2)]
+        w2_q = [quantize_half("w2", w2_dealt[half], half) for half in range(2)]
+        z = keep.tile([P, S, PACK], BF16, name="z", align_bytes=64)
+        nc.vector.tensor_tensor(
+            z[:].rearrange("p (c i) t -> p c t i", i=4),
+            factor[:].rearrange("p t (c i) -> p c t i", i=4),
+            st[:].rearrange("p t (c i) -> p c t i", i=4),
+            ALU.mult,
+        )
+        d_step = keep.tile([P, PACK, S], F32, name="d_step")
+        gate = keep.tile([P, PACK, S], F32, name="gate")
+        pair = [slice(2 * half, 2 * half + 2) for half in range(2)]
+        nc.vector.tensor_tensor(d_step[:, pair[0], :], d_far[:, pair[0], :], d_acc[0][:], ALU.subtract)
+        z_q = quantize("z", z[:].rearrange("p c t -> p (c t)"), S)
+        nc.vector.tensor_tensor(d_step[:, pair[1], :], d_far[:, pair[1], :], d_acc[1][:], ALU.subtract)
+        for half in range(2):
+            nc.scalar.activation(gate[:, pair[half], :], d_step[:, pair[half], :], ACT.Tanh, scale=0.5)
+        h_acc = [psum.tile([P, 2, S], F32, name="h_acc%d" % half) for half in range(2)]
+        for t in range(PACK):
+            product(h_acc[t // 2][:, t % 2, :], w2_q, t, z_q)
+        h_far = keep.tile([P, PACK, S], F32, name="h_far")
+        for t in range(PACK):
+            nc.vector.tensor_scalar(h_win[t][:, :S], h_acc[t // 2][:, t % 2, :], 0.5, None, ALU.mult)
+            fetch(h_far[:, t, :], h_win[t], n3_sb, ACT.Copy)
+
+        stay = keep.tile([P, PACK, S], F32, name="stay")
+        for half in range(2):
+            nc.vector.scalar_tensor_tensor(
+                stay[:, pair[half], :], gate[:, pair[half], :], 1.0, h_acc[half][:], ALU.subtract, ALU.mult
+            )
+        move = keep.tile([P, PACK, S], F32, name="move")
+        out_rows = out.rearrange("(p t) j -> p t j", t=PACK)
+        for t in range(PACK):
+            result = keep.tile([P, S], F32, name="result%d" % t)
+            nc.vector.scalar_tensor_tensor(move[:, t, :], gate[:, t, :], 1.0, h_far[:, t, :], ALU.add, ALU.mult)
+            nc.vector.scalar_tensor_tensor(result[:], stay[:, t, :], -0.5, move[:, t, :], ALU.mult, ALU.add)
+            nc.sync.dma_start(out_rows[:, t, :], result[:])

@@ -52,6 +52,13 @@ def tile_picked_latepullbhopn_none_p_kernel(
             )
             return dealt
 
+        def deal_lines(dealt, raw, half):
+            nc.vector.tensor_copy(
+                dealt.rearrange("p t (a b) j -> p t a j b", b=4),
+                raw[:].rearrange("p j (a t b) -> p t a j b", t=PACK, b=4)[:, 2 * half : 2 * half + 2],
+            )
+            return dealt
+
         def quantize(name, values, width):
             codes = keep.tile([P, width], U32, name=name + "_codes", align_bytes=64)
             scales = keep.tile([P, width], U8, name=name + "_scales", align_bytes=64)
@@ -75,17 +82,15 @@ def tile_picked_latepullbhopn_none_p_kernel(
             )
 
         def fetch(dst, window, places, func, **kwargs):
-            nc.scalar.activation(dst, window[:].indirect(places[:]), func, **kwargs)
+            nc.scalar.activation(dst, window[:].indirect(places), func, **kwargs)
 
         x_bytes = keep.tile([P, T], U8, name="x_bytes")
         nc.vector.memset(x_bytes[:].bitcast(I32), 0)
         gain = keep.tile([P, PACK], F32, name="gain")
         nc.sync.dma_start(gain[:], gn.rearrange("(p t) o -> p (t o)", t=PACK))
         w1_raw = load_weight("w1_raw", w1)
-        for q in range(4):
-            nc.sync.dma_start(
-                x_bytes[32 * q : 32 * q + 4, :].bitcast(I32), x_scales[0, 4 * q : 4 * q + 4, :].bitcast(I32)
-            )
+        for r in range(4):
+            nc.sync.dma_start(x_bytes[r:P:32, :].bitcast(I32), x_scales[0, r:16:4, :].bitcast(I32))
         offs_sb = load_list("offs_sb", offs)
         x_packed = keep.tile([P, T], U32, name="x_packed")
         nc.sync.dma_start(x_packed[:].bitcast(I32), x_words[0].rearrange("p n r -> p (n r)").bitcast(I32))
@@ -104,13 +109,13 @@ def tile_picked_latepullbhopn_none_p_kernel(
         gain_abs = keep.tile([P, PACK], F32, name="gain_abs")
         gain_floor = keep.tile([P, PACK], F32, name="gain_floor")
         gain_ln = keep.tile([P, PACK], F32, name="gain_ln")
-        gain_twice = keep.tile([P, PACK], F32, name="gain_twice")
+        gain_below = keep.tile([P, PACK], F32, name="gain_below")
         gain_sign = keep.tile([P, PACK], F32, name="gain_sign")
         nc.vector.scalar_tensor_tensor(gain_abs[:], gain[:], -1.0, gain[:], ALU.mult, ALU.max)
         nc.vector.tensor_scalar(gain_floor[:], gain_abs[:], LN_FLOOR, None, ALU.max)
         nc.scalar.activation(gain_ln[:], gain_floor[:], ACT.Ln)
-        nc.vector.tensor_scalar(gain_twice[:], gain[:], 0.0, 2.0, ALU.is_ge, ALU.mult)
-        nc.vector.tensor_scalar(gain_sign[:], gain_twice[:], -1.0, None, ALU.add)
+        nc.vector.tensor_scalar(gain_below[:], gain[:], 0.0, None, ALU.is_lt)
+        nc.vector.scalar_tensor_tensor(gain_sign[:], gain[:], 0.0, gain_below[:], ALU.is_gt, ALU.subtract)
 
         def pick(name, dtype, table, places):
             picked = keep.tile([P, S], dtype, name=name, align_bytes=64)
@@ -132,22 +137,18 @@ def tile_picked_latepullbhopn_none_p_kernel(
             product(y_acc[t][:], w1_q, t, (offs_words, offs_bytes))
         for t in range(PACK):
             nc.vector.tensor_scalar(y_win[t][:, :S], y_acc[t][:], gain_sign[:, t : t + 1], None, ALU.mult)
-            fetch(y_far[:, t, :], y_win[t], n1_sb, ACT.Copy)
-        last = PACK - 1
+            fetch(y_far[:, t, :], y_win[t], n1_sb[:], ACT.Copy)
         for t in range(PACK):
             nc.vector.tensor_tensor(st[:, t, :], y_win[t][:, :S], y_far[:, t, :], ALU.subtract)
-            if t < last:
-                nc.vector.scalar_tensor_tensor(ln_win[t][:, S:], st[:, t, :], -1.0, st[:, t, :], ALU.mult, ALU.max)
-            else:
-                nc.scalar.activation(ln_win[t][:, S:], st[:, t, :], ACT.Abs)
+            nc.vector.scalar_tensor_tensor(ln_win[t][:, S:], st[:, t, :], -1.0, st[:, t, :], ALU.mult, ALU.max)
             nc.scalar.activation(ln_win[t][:, :S], ln_win[t][:, S:], ACT.Ln, bias=0.5)
         factor = keep.tile([P, PACK, S], F32, name="factor")
         for t in range(PACK):
-            fetch(factor[:, t, :], ln_win[t], n2_sb, ACT.Exp, bias=gain_ln[:, t : t + 1], scale=-1.0)
+            fetch(factor[:, t, :], ln_win[t], n2_sb[:], ACT.Exp, bias=gain_ln[:, t : t + 1], scale=-1.0)
 
         two_words = pick("two_words", U32, x_packed, two_sb)
         w3_tile = dealt_tile("w3_tile", "y_far")
-        w3_dealt = [deal(w3_tile[:, 2 * half : 2 * half + 2], w3_raw, half, nc.vector.tensor_copy) for half in range(2)]
+        w3_dealt = [deal_lines(w3_tile[:, 2 * half : 2 * half + 2], w3_raw, half) for half in range(2)]
         w3_q = [quantize_half("w3", w3_dealt[half], half) for half in range(2)]
         d_acc = [psum.tile([P, 2, S], F32, name="d_acc%d" % half) for half in range(2)]
         for t in range(PACK):
@@ -155,10 +156,10 @@ def tile_picked_latepullbhopn_none_p_kernel(
         d_far = keep.tile([P, PACK, S], F32, name="d_far")
         for t in range(PACK):
             nc.vector.tensor_copy(d_win[t][:, :S], d_acc[t // 2][:, t % 2, :])
-            fetch(d_far[:, t, :], d_win[t], n4_sb, ACT.Copy)
+            fetch(d_far[:, t, :], d_win[t], n4_sb[:], ACT.Copy)
 
         w2_tile = dealt_tile("w2_tile", "y_far")
-        w2_dealt = [deal(w2_tile[:, 2 * half : 2 * half + 2], w2_raw, half, nc.vector.tensor_copy) for half in range(2)]
+        w2_dealt = [deal_lines(w2_tile[:, 2 * half : 2 * half + 2], w2_raw, half) for half in range(2)]
         w2_q = [quantize_half("w2", w2_dealt[half], half) for half in range(2)]
         z = keep.tile([P, S, PACK], BF16, name="z", align_bytes=64)
         nc.vector.tensor_tensor(
@@ -181,7 +182,9 @@ def tile_picked_latepullbhopn_none_p_kernel(
         h_far = keep.tile([P, PACK, S], F32, name="h_far")
         for t in range(PACK):
             nc.vector.tensor_scalar(h_win[t][:, :S], h_acc[t // 2][:, t % 2, :], 0.5, None, ALU.mult)
-            fetch(h_far[:, t, :], h_win[t], n3_sb, ACT.Copy)
+        pieces = [(t, 0, S) for t in range(PACK - 1)] + [(PACK - 1, 0, S // 2), (PACK - 1, S // 2, S)]
+        for t, lo, hi in pieces:
+            fetch(h_far[:, t, lo:hi], h_win[t], n3_sb[:, lo // 16 : hi // 16], ACT.Copy)
 
         stay = keep.tile([P, PACK, S], F32, name="stay")
         for half in range(2):
@@ -189,9 +192,11 @@ def tile_picked_latepullbhopn_none_p_kernel(
                 stay[:, pair[half], :], gate[:, pair[half], :], 1.0, h_acc[half][:], ALU.subtract, ALU.mult
             )
         move = keep.tile([P, PACK, S], F32, name="move")
-        out_rows = out.rearrange("(p t) j -> p t j", t=PACK)
-        for t in range(PACK):
-            result = keep.tile([P, S], F32, name="result%d" % t)
-            nc.vector.scalar_tensor_tensor(move[:, t, :], gate[:, t, :], 1.0, h_far[:, t, :], ALU.add, ALU.mult)
-            nc.vector.scalar_tensor_tensor(result[:], stay[:, t, :], -0.5, move[:, t, :], ALU.mult, ALU.add)
-            nc.sync.dma_start(out_rows[:, t, :], result[:])
+        out_rows = out.rearrange("(a t b) j -> t a b j", t=PACK, b=4)
+        for t, lo, hi in pieces:
+            result = keep.tile([P, hi - lo], F32, name="result%d_%d" % (t, lo))
+            nc.vector.scalar_tensor_tensor(
+                move[:, t, lo:hi], gate[:, t, lo:hi], 1.0, h_far[:, t, lo:hi], ALU.add, ALU.mult
+            )
+            nc.vector.scalar_tensor_tensor(result[:], stay[:, t, lo:hi], -0.5, move[:, t, lo:hi], ALU.mult, ALU.add)
+            nc.sync.dma_start(out_rows[t][:, :, lo:hi], result[:])

@@ -3,7 +3,7 @@ from contextlib import ExitStack
 import concourse.mybir as mybir
 
 K, T, S, N, H = 512, 2048, 256, 512, 512
-FLOPS = 3 * 2 * 512 * 512 * S
+FLOPS = 2 * S * (K * H + H * N + K * N)
 
 F32 = mybir.dt.float32
 BF16 = mybir.dt.bfloat16
@@ -17,8 +17,11 @@ ACT = mybir.ActivationFunctionType
 
 P = 128
 PACK = 4
+LIST_ROWS = 16
+QUADRANT = 32
 WINDOW = 2 * S
-LN_FLOOR = 2.0 ** -64
+LN_FLOOR = 2.0**-64
+PAIRS = [slice(0, 2), slice(2, 4)]
 
 
 def tile_picked_latepullbhopn_none_p_kernel(
@@ -30,46 +33,47 @@ def tile_picked_latepullbhopn_none_p_kernel(
         psum = ctx.enter_context(tc.psum_pool(name="psum", bufs=1))
 
         def load_list(name, src):
-            tile = keep.tile([P, S // 16], U16, name=name)
+            tile = keep.tile([P, S // LIST_ROWS], U16, name=name)
             nc.sync.dma_start(tile[:], src)
             return tile
 
         def load_weight(name, src):
-            raw = keep.tile([P, PACK, 512], F32, name=name)
+            raw = keep.tile([P, PACK, PACK * P], F32, name=name)
             nc.sync.dma_start(raw[:], src.rearrange("(p j) c -> p j c", j=PACK))
             return raw
 
         def windows(name):
             return [keep.tile([P, WINDOW], F32, name="%s%d" % (name, t)) for t in range(PACK)]
 
-        def dealt_tile(name, tag):
-            return keep.tile([P, PACK, P, PACK], BF16, name=name, tag=tag, align_bytes=64)
-
-        def deal(dealt, raw, half, copy):
+        def order_for_y(grouped, raw, pair, copy):
             copy(
-                dealt.rearrange("p t m j -> p m j t"),
-                raw[:].rearrange("p j (m t) -> p m j t", t=PACK)[:, :, :, 2 * half : 2 * half + 2],
+                grouped.rearrange("p t m j -> p m j t"),
+                raw[:].rearrange("p j (m t) -> p m j t", t=PACK)[:, :, :, pair],
             )
-            return dealt
 
-        def deal_lines(dealt, raw, half):
+        def order_for_out(grouped, raw, pair):
             nc.vector.tensor_copy(
-                dealt.rearrange("p t (a b) j -> p t a j b", b=4),
-                raw[:].rearrange("p j (a t b) -> p t a j b", t=PACK, b=4)[:, 2 * half : 2 * half + 2],
+                grouped.rearrange("p t (a b) j -> p t a j b", b=PACK),
+                raw[:].rearrange("p j (a t b) -> p t a j b", t=PACK, b=PACK)[:, pair],
             )
-            return dealt
 
-        def quantize(name, values, width):
-            codes = keep.tile([P, width], U32, name=name + "_codes", align_bytes=64)
-            scales = keep.tile([P, width], U8, name=name + "_scales", align_bytes=64)
+        def quantize(name, values, words):
+            codes = keep.tile([P, words], U32, name=name + "_codes", align_bytes=64)
+            scales = keep.tile([P, words], U8, name=name + "_scales", align_bytes=64)
             nc.vector.quantize_mx(out=codes[:].bitcast(FP8X4), scales=scales[:], in_=values)
             return codes, scales
 
-        def quantize_half(name, dealt, half):
-            return quantize("%s_%d" % (name, half), dealt.rearrange("p t m j -> p (t m j)"), 2 * P)
+        def quantize_pair(name, grouped):
+            return quantize(name, grouped.rearrange("p t m j -> p (t m j)"), 2 * P)
 
-        def product(acc, halves, t, moving):
-            codes, scales = halves[t // 2]
+        def quantize_late_weight(name, raw):
+            grouped = keep.tile([P, PACK, P, PACK], BF16, name=name + "_grouped", tag="y_far", align_bytes=64)
+            for pair in PAIRS:
+                order_for_out(grouped[:, pair], raw, pair)
+            return [quantize_pair("%s_%d" % (name, u), grouped[:, pair]) for u, pair in enumerate(PAIRS)]
+
+        def product(acc, weight, t, moving):
+            codes, scales = weight[t // 2]
             cols = slice(t % 2 * P, (t % 2 + 1) * P)
             nc.tensor.matmul_mx(
                 out=acc,
@@ -81,6 +85,11 @@ def tile_picked_latepullbhopn_none_p_kernel(
                 stop=True,
             )
 
+        def pick(name, dtype, table, places):
+            picked = keep.tile([P, S], dtype, name=name, align_bytes=64)
+            nc.vector.tensor_copy(picked[:], table[:].indirect(places[:]))
+            return picked
+
         def fetch(dst, window, places, func, **kwargs):
             nc.scalar.activation(dst, window[:].indirect(places), func, **kwargs)
 
@@ -89,8 +98,8 @@ def tile_picked_latepullbhopn_none_p_kernel(
         gain = keep.tile([P, PACK], F32, name="gain")
         nc.sync.dma_start(gain[:], gn.rearrange("(p t) o -> p (t o)", t=PACK))
         w1_raw = load_weight("w1_raw", w1)
-        for r in range(4):
-            nc.sync.dma_start(x_bytes[r:P:32, :].bitcast(I32), x_scales[0, r:16:4, :].bitcast(I32))
+        for r in range(PACK):
+            nc.sync.dma_start(x_bytes[r:P:QUADRANT, :].bitcast(I32), x_scales[0, r : K // 32 : PACK, :].bitcast(I32))
         offs_sb = load_list("offs_sb", offs)
         x_packed = keep.tile([P, T], U32, name="x_packed")
         nc.sync.dma_start(x_packed[:].bitcast(I32), x_words[0].rearrange("p n r -> p (n r)").bitcast(I32))
@@ -102,8 +111,9 @@ def tile_picked_latepullbhopn_none_p_kernel(
         n4_sb = load_list("n4_sb", n4)
         n3_sb = load_list("n3_sb", n3)
 
-        y_win, ln_win, d_win, h_win = windows("y_win"), windows("ln_win"), windows("d_win"), windows("h_win")
-        for win in y_win + d_win + h_win:
+        y_win, ln_win = windows("y_win"), windows("ln_win")
+        d_win, h_win = y_win, ln_win
+        for win in y_win:
             nc.vector.memset(win[:, S:], 0.0)
 
         gain_abs = keep.tile([P, PACK], F32, name="gain_abs")
@@ -117,17 +127,13 @@ def tile_picked_latepullbhopn_none_p_kernel(
         nc.vector.tensor_scalar(gain_below[:], gain[:], 0.0, None, ALU.is_lt)
         nc.vector.scalar_tensor_tensor(gain_sign[:], gain[:], 0.0, gain_below[:], ALU.is_gt, ALU.subtract)
 
-        def pick(name, dtype, table, places):
-            picked = keep.tile([P, S], dtype, name=name, align_bytes=64)
-            nc.vector.tensor_copy(picked[:], table[:].indirect(places[:]))
-            return picked
-
-        w1_dealt = []
-        for half, copy in enumerate((nc.vector.tensor_copy, nc.scalar.copy)):
-            dealt = keep.tile([P, 2, P, PACK], BF16, name="w1_dealt%d" % half, align_bytes=64)
-            w1_dealt.append(deal(dealt[:], w1_raw, half, copy))
+        w1_grouped = []
+        for u, copy in enumerate((nc.vector.tensor_copy, nc.scalar.copy)):
+            grouped = keep.tile([P, 2, P, PACK], BF16, name="w1_grouped%d" % u, align_bytes=64)
+            order_for_y(grouped[:], w1_raw, PAIRS[u], copy)
+            w1_grouped.append(grouped)
         offs_bytes = pick("offs_bytes", U8, x_bytes, offs_sb)
-        w1_q = [quantize_half("w1", w1_dealt[half], half) for half in range(2)]
+        w1_q = [quantize_pair("w1_%d" % u, grouped[:]) for u, grouped in enumerate(w1_grouped)]
         two_bytes = pick("two_bytes", U8, x_bytes, two_sb)
         offs_words = pick("offs_words", U32, x_packed, offs_sb)
         y_acc = [psum.tile([P, S], F32, name="y_acc%d" % t) for t in range(PACK)]
@@ -138,6 +144,7 @@ def tile_picked_latepullbhopn_none_p_kernel(
         for t in range(PACK):
             nc.vector.tensor_scalar(y_win[t][:, :S], y_acc[t][:], gain_sign[:, t : t + 1], None, ALU.mult)
             fetch(y_far[:, t, :], y_win[t], n1_sb[:], ACT.Copy)
+
         for t in range(PACK):
             nc.vector.tensor_tensor(st[:, t, :], y_win[t][:, :S], y_far[:, t, :], ALU.subtract)
             nc.vector.scalar_tensor_tensor(ln_win[t][:, S:], st[:, t, :], -1.0, st[:, t, :], ALU.mult, ALU.max)
@@ -147,10 +154,8 @@ def tile_picked_latepullbhopn_none_p_kernel(
             fetch(factor[:, t, :], ln_win[t], n2_sb[:], ACT.Exp, bias=gain_ln[:, t : t + 1], scale=-1.0)
 
         two_words = pick("two_words", U32, x_packed, two_sb)
-        w3_tile = dealt_tile("w3_tile", "y_far")
-        w3_dealt = [deal_lines(w3_tile[:, 2 * half : 2 * half + 2], w3_raw, half) for half in range(2)]
-        w3_q = [quantize_half("w3", w3_dealt[half], half) for half in range(2)]
-        d_acc = [psum.tile([P, 2, S], F32, name="d_acc%d" % half) for half in range(2)]
+        w3_q = quantize_late_weight("w3", w3_raw)
+        d_acc = [psum.tile([P, 2, S], F32, name="d_acc%d" % u) for u in range(2)]
         for t in range(PACK):
             product(d_acc[t // 2][:, t % 2, :], w3_q, t, (two_words, two_bytes))
         d_far = keep.tile([P, PACK, S], F32, name="d_far")
@@ -158,25 +163,23 @@ def tile_picked_latepullbhopn_none_p_kernel(
             nc.vector.tensor_copy(d_win[t][:, :S], d_acc[t // 2][:, t % 2, :])
             fetch(d_far[:, t, :], d_win[t], n4_sb[:], ACT.Copy)
 
-        w2_tile = dealt_tile("w2_tile", "y_far")
-        w2_dealt = [deal_lines(w2_tile[:, 2 * half : 2 * half + 2], w2_raw, half) for half in range(2)]
-        w2_q = [quantize_half("w2", w2_dealt[half], half) for half in range(2)]
+        w2_q = quantize_late_weight("w2", w2_raw)
         z = keep.tile([P, S, PACK], BF16, name="z", align_bytes=64)
         nc.vector.tensor_tensor(
-            z[:].rearrange("p (c i) t -> p c t i", i=4),
-            factor[:].rearrange("p t (c i) -> p c t i", i=4),
-            st[:].rearrange("p t (c i) -> p c t i", i=4),
+            z[:].rearrange("p (c i) t -> p c t i", i=PACK),
+            factor[:].rearrange("p t (c i) -> p c t i", i=PACK),
+            st[:].rearrange("p t (c i) -> p c t i", i=PACK),
             ALU.mult,
         )
         d_step = keep.tile([P, PACK, S], F32, name="d_step")
         gate = keep.tile([P, PACK, S], F32, name="gate")
-        pair = [slice(2 * half, 2 * half + 2) for half in range(2)]
-        nc.vector.tensor_tensor(d_step[:, pair[0], :], d_far[:, pair[0], :], d_acc[0][:], ALU.subtract)
+        nc.vector.tensor_tensor(d_step[:, PAIRS[0], :], d_far[:, PAIRS[0], :], d_acc[0][:], ALU.subtract)
         z_q = quantize("z", z[:].rearrange("p c t -> p (c t)"), S)
-        nc.vector.tensor_tensor(d_step[:, pair[1], :], d_far[:, pair[1], :], d_acc[1][:], ALU.subtract)
-        for half in range(2):
-            nc.scalar.activation(gate[:, pair[half], :], d_step[:, pair[half], :], ACT.Tanh, scale=0.5)
-        h_acc = [psum.tile([P, 2, S], F32, name="h_acc%d" % half) for half in range(2)]
+        nc.vector.tensor_tensor(d_step[:, PAIRS[1], :], d_far[:, PAIRS[1], :], d_acc[1][:], ALU.subtract)
+        for pair in PAIRS:
+            nc.scalar.activation(gate[:, pair, :], d_step[:, pair, :], ACT.Tanh, scale=0.5)
+
+        h_acc = [psum.tile([P, 2, S], F32, name="h_acc%d" % u) for u in range(2)]
         for t in range(PACK):
             product(h_acc[t // 2][:, t % 2, :], w2_q, t, z_q)
         h_far = keep.tile([P, PACK, S], F32, name="h_far")
@@ -184,15 +187,13 @@ def tile_picked_latepullbhopn_none_p_kernel(
             nc.vector.tensor_scalar(h_win[t][:, :S], h_acc[t // 2][:, t % 2, :], 0.5, None, ALU.mult)
         pieces = [(t, 0, S) for t in range(PACK - 1)] + [(PACK - 1, 0, S // 2), (PACK - 1, S // 2, S)]
         for t, lo, hi in pieces:
-            fetch(h_far[:, t, lo:hi], h_win[t], n3_sb[:, lo // 16 : hi // 16], ACT.Copy)
+            fetch(h_far[:, t, lo:hi], h_win[t], n3_sb[:, lo // LIST_ROWS : hi // LIST_ROWS], ACT.Copy)
 
         stay = keep.tile([P, PACK, S], F32, name="stay")
-        for half in range(2):
-            nc.vector.scalar_tensor_tensor(
-                stay[:, pair[half], :], gate[:, pair[half], :], 1.0, h_acc[half][:], ALU.subtract, ALU.mult
-            )
+        for u, pair in enumerate(PAIRS):
+            nc.vector.scalar_tensor_tensor(stay[:, pair, :], gate[:, pair, :], 1.0, h_acc[u][:], ALU.subtract, ALU.mult)
         move = keep.tile([P, PACK, S], F32, name="move")
-        out_rows = out.rearrange("(a t b) j -> t a b j", t=PACK, b=4)
+        out_rows = out.rearrange("(a t b) j -> t a b j", t=PACK, b=PACK)
         for t, lo, hi in pieces:
             result = keep.tile([P, hi - lo], F32, name="result%d_%d" % (t, lo))
             nc.vector.scalar_tensor_tensor(

from contextlib import ExitStack

import concourse.mybir as mybir

K, T, S, N, H = 512, 2048, 256, 512, 512
FLOPS = 2 * S * (K * H + H * N + K * N)

F32 = mybir.dt.float32
BF16 = mybir.dt.bfloat16
I32 = mybir.dt.int32
U32 = mybir.dt.uint32
U16 = mybir.dt.uint16
U8 = mybir.dt.uint8
FP8X4 = mybir.dt.float8_e4m3fn_x4
ALU = mybir.AluOpType
ACT = mybir.ActivationFunctionType

P = 128
PACK = 4
LIST_ROWS = 16
QUADRANT = 32
WINDOW = 2 * S
LN_FLOOR = 2.0**-64
PAIRS = [slice(0, 2), slice(2, 4)]


def tile_picked_latepullbhopn_none_p_kernel(
    tc, x_words, x_scales, w1, gn, w2, w3, offs, n1, n2, two, n3, n4, out
):
    nc = tc.nc
    with ExitStack() as ctx:
        keep = ctx.enter_context(tc.tile_pool(name="keep", bufs=1))
        psum = ctx.enter_context(tc.psum_pool(name="psum", bufs=1))

        def load_list(name, src):
            tile = keep.tile([P, S // LIST_ROWS], U16, name=name)
            nc.sync.dma_start(tile[:], src)
            return tile

        def load_weight(name, src):
            raw = keep.tile([P, PACK, PACK * P], F32, name=name)
            nc.sync.dma_start(raw[:], src.rearrange("(p j) c -> p j c", j=PACK))
            return raw

        def windows(name):
            return [keep.tile([P, WINDOW], F32, name="%s%d" % (name, t)) for t in range(PACK)]

        def order_for_y(grouped, raw, pair, copy):
            copy(
                grouped.rearrange("p t m j -> p m j t"),
                raw[:].rearrange("p j (m t) -> p m j t", t=PACK)[:, :, :, pair],
            )

        def order_for_out(grouped, raw, pair):
            nc.vector.tensor_copy(
                grouped.rearrange("p t (a b) j -> p t a j b", b=PACK),
                raw[:].rearrange("p j (a t b) -> p t a j b", t=PACK, b=PACK)[:, pair],
            )

        def quantize(name, values, words):
            codes = keep.tile([P, words], U32, name=name + "_codes", align_bytes=64)
            scales = keep.tile([P, words], U8, name=name + "_scales", align_bytes=64)
            nc.vector.quantize_mx(out=codes[:].bitcast(FP8X4), scales=scales[:], in_=values)
            return codes, scales

        def quantize_pair(name, grouped):
            return quantize(name, grouped.rearrange("p t m j -> p (t m j)"), 2 * P)

        def quantize_late_weight(name, raw):
            grouped = keep.tile([P, PACK, P, PACK], BF16, name=name + "_grouped", tag="y_far", align_bytes=64)
            for pair in PAIRS:
                order_for_out(grouped[:, pair], raw, pair)
            return [quantize_pair("%s_%d" % (name, u), grouped[:, pair]) for u, pair in enumerate(PAIRS)]

        def product(acc, weight, t, moving):
            codes, scales = weight[t // 2]
            cols = slice(t % 2 * P, (t % 2 + 1) * P)
            nc.tensor.matmul_mx(
                out=acc,
                lhsT=codes[:, cols].bitcast(FP8X4),
                lhsT_scale=scales[:, cols],
                rhs=moving[0][:].bitcast(FP8X4),
                rhs_scale=moving[1][:],
                start=True,
                stop=True,
            )

        def pick(name, dtype, table, places):
            picked = keep.tile([P, S], dtype, name=name, align_bytes=64)
            nc.vector.tensor_copy(picked[:], table[:].indirect(places[:]))
            return picked

        def fetch(dst, window, places, func, **kwargs):
            nc.scalar.activation(dst, window[:].indirect(places), func, **kwargs)

        x_bytes = keep.tile([P, T], U8, name="x_bytes")
        nc.vector.memset(x_bytes[:].bitcast(I32), 0)
        gain = keep.tile([P, PACK], F32, name="gain")
        nc.sync.dma_start(gain[:], gn.rearrange("(p t) o -> p (t o)", t=PACK))
        w1_raw = load_weight("w1_raw", w1)
        for r in range(PACK):
            nc.sync.dma_start(x_bytes[r:P:QUADRANT, :].bitcast(I32), x_scales[0, r : K // 32 : PACK, :].bitcast(I32))
        offs_sb = load_list("offs_sb", offs)
        x_packed = keep.tile([P, T], U32, name="x_packed")
        nc.sync.dma_start(x_packed[:].bitcast(I32), x_words[0].rearrange("p n r -> p (n r)").bitcast(I32))
        two_sb = load_list("two_sb", two)
        n1_sb = load_list("n1_sb", n1)
        w3_raw = load_weight("w3_raw", w3)
        w2_raw = load_weight("w2_raw", w2)
        n2_sb = load_list("n2_sb", n2)
        n4_sb = load_list("n4_sb", n4)
        n3_sb = load_list("n3_sb", n3)

        y_win, ln_win = windows("y_win"), windows("ln_win")
        d_win, h_win = y_win, ln_win
        for win in y_win:
            nc.vector.memset(win[:, S:], 0.0)

        gain_abs = keep.tile([P, PACK], F32, name="gain_abs")
        gain_floor = keep.tile([P, PACK], F32, name="gain_floor")
        gain_ln = keep.tile([P, PACK], F32, name="gain_ln")
        gain_below = keep.tile([P, PACK], F32, name="gain_below")
        gain_sign = keep.tile([P, PACK], F32, name="gain_sign")
        nc.vector.scalar_tensor_tensor(gain_abs[:], gain[:], -1.0, gain[:], ALU.mult, ALU.max)
        nc.vector.tensor_scalar(gain_floor[:], gain_abs[:], LN_FLOOR, None, ALU.max)
        nc.scalar.activation(gain_ln[:], gain_floor[:], ACT.Ln)
        nc.vector.tensor_scalar(gain_below[:], gain[:], 0.0, None, ALU.is_lt)
        nc.vector.scalar_tensor_tensor(gain_sign[:], gain[:], 0.0, gain_below[:], ALU.is_gt, ALU.subtract)

        w1_grouped = []
        for u, copy in enumerate((nc.vector.tensor_copy, nc.scalar.copy)):
            grouped = keep.tile([P, 2, P, PACK], BF16, name="w1_grouped%d" % u, align_bytes=64)
            order_for_y(grouped[:], w1_raw, PAIRS[u], copy)
            w1_grouped.append(grouped)
        offs_bytes = pick("offs_bytes", U8, x_bytes, offs_sb)
        w1_q = [quantize_pair("w1_%d" % u, grouped[:]) for u, grouped in enumerate(w1_grouped)]
        two_bytes = pick("two_bytes", U8, x_bytes, two_sb)
        offs_words = pick("offs_words", U32, x_packed, offs_sb)
        y_acc = [psum.tile([P, S], F32, name="y_acc%d" % t) for t in range(PACK)]
        y_far = keep.tile([P, PACK, S], F32, name="y_far", tag="y_far", align_bytes=64)
        st = keep.tile([P, PACK, S], F32, name="st")
        for t in range(PACK):
            product(y_acc[t][:], w1_q, t, (offs_words, offs_bytes))
        for t in range(PACK):
            nc.vector.tensor_scalar(y_win[t][:, :S], y_acc[t][:], gain_sign[:, t : t + 1], None, ALU.mult)
            fetch(y_far[:, t, :], y_win[t], n1_sb[:], ACT.Copy)

        for t in range(PACK):
            nc.vector.tensor_tensor(st[:, t, :], y_win[t][:, :S], y_far[:, t, :], ALU.subtract)
            nc.vector.scalar_tensor_tensor(ln_win[t][:, S:], st[:, t, :], -1.0, st[:, t, :], ALU.mult, ALU.max)
            nc.scalar.activation(ln_win[t][:, :S], ln_win[t][:, S:], ACT.Ln, bias=0.5)
        factor = keep.tile([P, PACK, S], F32, name="factor")
        for t in range(PACK):
            fetch(factor[:, t, :], ln_win[t], n2_sb[:], ACT.Exp, bias=gain_ln[:, t : t + 1], scale=-1.0)

        two_words = pick("two_words", U32, x_packed, two_sb)
        w3_q = quantize_late_weight("w3", w3_raw)
        d_acc = [psum.tile([P, 2, S], F32, name="d_acc%d" % u) for u in range(2)]
        for t in range(PACK):
            product(d_acc[t // 2][:, t % 2, :], w3_q, t, (two_words, two_bytes))
        d_far = keep.tile([P, PACK, S], F32, name="d_far")
        for t in range(PACK):
            nc.vector.tensor_copy(d_win[t][:, :S], d_acc[t // 2][:, t % 2, :])
            fetch(d_far[:, t, :], d_win[t], n4_sb[:], ACT.Copy)

        w2_q = quantize_late_weight("w2", w2_raw)
        z = keep.tile([P, S, PACK], BF16, name="z", align_bytes=64)
        nc.vector.tensor_tensor(
            z[:].rearrange("p (c i) t -> p c t i", i=PACK),
            factor[:].rearrange("p t (c i) -> p c t i", i=PACK),
            st[:].rearrange("p t (c i) -> p c t i", i=PACK),
            ALU.mult,
        )
        d_step = keep.tile([P, PACK, S], F32, name="d_step")
        gate = keep.tile([P, PACK, S], F32, name="gate")
        nc.vector.tensor_tensor(d_step[:, PAIRS[0], :], d_far[:, PAIRS[0], :], d_acc[0][:], ALU.subtract)
        z_q = quantize("z", z[:].rearrange("p c t -> p (c t)"), S)
        nc.vector.tensor_tensor(d_step[:, PAIRS[1], :], d_far[:, PAIRS[1], :], d_acc[1][:], ALU.subtract)
        for pair in PAIRS:
            nc.scalar.activation(gate[:, pair, :], d_step[:, pair, :], ACT.Tanh, scale=0.5)

        h_acc = [psum.tile([P, 2, S], F32, name="h_acc%d" % u) for u in range(2)]
        for t in range(PACK):
            product(h_acc[t // 2][:, t % 2, :], w2_q, t, z_q)
        h_far = keep.tile([P, PACK, S], F32, name="h_far")
        for t in range(PACK):
            nc.vector.tensor_scalar(h_win[t][:, :S], h_acc[t // 2][:, t % 2, :], 0.5, None, ALU.mult)
        pieces = [(t, 0, S) for t in range(PACK - 1)] + [(PACK - 1, 0, S // 2), (PACK - 1, S // 2, S)]
        for t, lo, hi in pieces:
            fetch(h_far[:, t, lo:hi], h_win[t], n3_sb[:, lo // LIST_ROWS : hi // LIST_ROWS], ACT.Copy)

        stay = keep.tile([P, PACK, S], F32, name="stay")
        for u, pair in enumerate(PAIRS):
            nc.vector.scalar_tensor_tensor(stay[:, pair, :], gate[:, pair, :], 1.0, h_acc[u][:], ALU.subtract, ALU.mult)
        move = keep.tile([P, PACK, S], F32, name="move")
        out_rows = out.rearrange("(a t b) j -> t a b j", t=PACK, b=PACK)
        for t, lo, hi in pieces:
            result = keep.tile([P, hi - lo], F32, name="result%d_%d" % (t, lo))
            nc.vector.scalar_tensor_tensor(
                move[:, t, lo:hi], gate[:, t, lo:hi], 1.0, h_far[:, t, lo:hi], ALU.add, ALU.mult
            )
            nc.vector.scalar_tensor_tensor(result[:], stay[:, t, lo:hi], -0.5, move[:, t, lo:hi], ALU.mult, ALU.add)
            nc.sync.dma_start(out_rows[t][:, :, lo:hi], result[:])
